import numpy as np, ml_dtypes
CORES = [66,74,82,90,194,202,210,218]
N = 8
QP = 32
def setup_inputs(rng):
    return {"q": rng.standard_normal((N, 128, QP), dtype=np.float32).astype(ml_dtypes.bfloat16), "k": rng.standard_normal((N, 128, 128), dtype=np.float32).astype(ml_dtypes.bfloat16), "v": rng.standard_normal((N, 128, 128), dtype=np.float32).astype(ml_dtypes.bfloat16), "b": (8 * rng.standard_normal((N, 128, N * QP), dtype=np.float32)).astype(ml_dtypes.bfloat16)}
def setup_inputs_big(rng):
    d = setup_inputs(rng)
    for k in ("q", "k", "v", "b"): d[k] = (d[k].astype(np.float32) * 1024.0).astype(d[k].dtype)
    return d
def setup_inputs_small(rng):
    d = setup_inputs(rng)
    for k in ("q", "k", "v", "b"): d[k] = (d[k].astype(np.float32) * (1 / 1024.0)).astype(d[k].dtype)
    return d
def setup_inputs_apart(rng):
    d = setup_inputs(rng)
    f = (10.0 ** rng.permutation(np.linspace(-1.5, 1.5, N))).astype(np.float32).reshape(N, 1, 1)
    for k in ("q", "k", "v", "b"): d[k] = (d[k].astype(np.float32) * f).astype(d[k].dtype)
    return d
def reference(q, k, v, b):
    Q, K, V, B = q.astype(np.float64), k.astype(np.float64), v.astype(np.float64), b.astype(np.float64)
    y = np.zeros((N, 128, QP))
    for r in range(N):
        for j in range(N):
            y[r] += V[j].T @ np.maximum(K[j].T @ Q[r] + B[r][:, QP * j:QP * j + QP], 0.0)
    return {"y": y.astype(ml_dtypes.bfloat16 if q.dtype != np.float64 else np.float64)}

@@ -1,0 +1,96 @@
+from concourse.bass import DstId, RemoteDMATransfer
+from concourse.mybir import AluOpType
+
+N = 8
+QP = 32
+KP = 128
+W = 2 * KP
+
+SCRATCH = {
+    "kv": ("sbuf", [128, N * W], "bfloat16"),
+    "qs": ("sbuf", [128, QP], "bfloat16"),
+    "bs": ("sbuf", [128, N * QP], "bfloat16"),
+    "nb": ("sbuf", [128, N * QP], "bfloat16"),
+    "zero": ("sbuf", [128, N * QP], "bfloat16"),
+    "s": ("sbuf", [128, N * QP], "bfloat16"),
+    "yo": ("sbuf", [128, QP], "bfloat16"),
+    "p0": ("psum", [128, 512], "float32"),
+    "p1": ("psum", [128, 512], "float32"),
+    "acc": ("psum", [128, 512], "float32"),
+}
+SEMAPHORES = ["ld_kv", "ld_qb", "sent", "vz", "vnb", "pe1", "vmax", "pe2", "vy", "st"] + ["a%d" % j for j in range(N)]
+
+
+def rank_program(g, core, T, topo):
+    rank = T.rank_of(core)
+    if rank is None:
+        return
+    sem = T.sem
+    pe, ve = g.tensor, g.vector
+
+    def k_of(j):
+        return T.kv[:, j * W:j * W + KP]
+
+    def v_of(j):
+        return T.kv[:, j * W + KP:(j + 1) * W]
+
+    def cols(t, j):
+        return t[:, j * QP:(j + 1) * QP]
+
+    def links(a, c):
+        return 1 if (topo.mates(a, c) or topo.same_plane(a, c)) else 2
+
+    steps = sorted(range(1, N), key=lambda t: (-links(core, T.cores[rank ^ t]), t))
+    partners = [rank ^ t for t in steps]
+
+    g.sync.dma_start(k_of(rank), T.k[:]).then_inc(sem.ld_kv, 16)
+    g.scalar.dma_start(v_of(rank), T.v[:]).then_inc(sem.ld_kv, 16)
+    g.sync.dma_start(T.qs[:], T.q[:]).then_inc(sem.ld_qb, 16)
+    g.scalar.dma_start(T.bs[:], T.b[:]).then_inc(sem.ld_qb, 16)
+
+    mask = topo.mask(core, T.cores[partners[0]])
+    for j in partners:
+        mask &= topo.mask(core, T.cores[j])
+    eng = bin(mask).count("1")
+    own = T.kv[:, rank * W:(rank + 1) * W]
+    ids = []
+    for j in partners:
+        rid, pid = topo.addr(T.cores[j], core)
+        ids.append(DstId(rid=rid, pnc=pid))
+    g.wait_ge(sem.ld_kv, 32)
+    g.remote_dma_fused(
+        [RemoteDMATransfer(dst_ids=ids, dma_engine_mask=mask, remote_sem=sem["a%d" % rank],
+                           srcs=[own], dsts=[own for _ in partners])],
+        local_sem=sem.sent)
+
+    order = [rank] + partners
+    banks = [T.p0, T.p1]
+    acc = T.acc[:, 0:QP]
+    ve.memset(T.zero[:], 0.0).then_inc(sem.vz, 1)
+    ve.wait_ge(sem.vz, 1)
+    ve.wait_ge(sem.ld_qb, 32)
+    ve.tensor_tensor(T.nb[:], T.zero[:], T.bs[:], AluOpType.subtract).then_inc(sem.vnb, 1)
+    ve.wait_ge(sem.vnb, 1)
+    for i, j in enumerate(order):
+        ve.wait_ge(sem.pe1, i + 1)
+        ve.tensor_tensor(cols(T.s, i), banks[i % 2][:, 0:QP], cols(T.nb, j), AluOpType.max).then_inc(sem.vmax, 1)
+    ve.wait_ge(sem.pe2, 1)
+    ve.tensor_copy(T.yo[:], acc).then_inc(sem.vy, 1)
+
+    pe.wait_ge(sem.ld_kv, 32)
+    pe.wait_ge(sem.ld_qb, 32)
+    for i, j in enumerate(order):
+        if i > 0:
+            pe.wait_ge(sem["a%d" % j], eng)
+        pe.matmul(banks[i % 2][:, 0:QP], k_of(j), T.qs[:], start=True, stop=True).then_inc(sem.pe1, 1)
+        pe.matmul(acc, v_of(j), cols(T.bs, j), start=(i == 0), stop=False)
+        if i > 0:
+            pe.wait_ge(sem.vmax, i)
+            pe.matmul(acc, v_of(order[i - 1]), cols(T.s, i - 1), start=False, stop=False)
+    pe.wait_ge(sem.vmax, N)
+    pe.matmul(acc, v_of(order[N - 1]), cols(T.s, N - 1), start=False, stop=True).then_inc(sem.pe2, 1)
+
+    g.sync.wait_ge(sem.vy, 1)
+    g.sync.dma_start(T.y[:], T.yo[:]).then_inc(sem.st, 16)
+    g.sync.wait_ge(sem.st, 16)
+    g.wait_ge(sem.sent, eng)

@@ -8,17 +8,22 @@ W = 2 * KP
 
 SCRATCH = {
     "kv": ("sbuf", [128, N * W], "bfloat16"),
+    "kd": ("dram", [128, KP], "bfloat16"),
     "qs": ("sbuf", [128, QP], "bfloat16"),
     "bs": ("sbuf", [128, N * QP], "bfloat16"),
     "nb": ("sbuf", [128, N * QP], "bfloat16"),
     "zero": ("sbuf", [128, N * QP], "bfloat16"),
     "s": ("sbuf", [128, N * QP], "bfloat16"),
+    "tl": ("sbuf", [128, QP], "float32"),
+    "sl": ("sbuf", [128, QP], "bfloat16"),
     "yo": ("sbuf", [128, QP], "bfloat16"),
     "p0": ("psum", [128, 512], "float32"),
     "p1": ("psum", [128, 512], "float32"),
+    "pl": ("psum", [128, 512], "float32"),
     "acc": ("psum", [128, 512], "float32"),
 }
-SEMAPHORES = ["ld_kv", "ld_qb", "sent", "vz", "vnb", "pe1", "vmax", "pe2", "vy", "st"] + ["a%d" % j for j in range(N)]
+SEMAPHORES = ["ld_kd", "ld_k", "ld_v", "ld_qb", "sent", "vz", "vnb", "pe1", "vmax", "peL", "vt", "vL", "pe2", "vy", "st",
+              "ak", "av"] + ["a%d" % j for j in range(N)]
 
 
 def rank_program(g, core, T, topo):
@@ -42,9 +47,11 @@ def rank_program(g, core, T, topo):
 
     steps = sorted(range(1, N), key=lambda t: (-links(core, T.cores[rank ^ t]), t))
     partners = [rank ^ t for t in steps]
+    whole, last = partners[:-1], partners[-1]
 
-    g.sync.dma_start(k_of(rank), T.k[:]).then_inc(sem.ld_kv, 16)
-    g.scalar.dma_start(v_of(rank), T.v[:]).then_inc(sem.ld_kv, 16)
+    g.sync.dma_start(T.kd[:], T.k[:]).then_inc(sem.ld_kd, 16)
+    g.scalar.dma_start(k_of(rank), T.k[:]).then_inc(sem.ld_k, 16)
+    g.sync.dma_start(v_of(rank), T.v[:]).then_inc(sem.ld_v, 16)
     g.sync.dma_start(T.qs[:], T.q[:]).then_inc(sem.ld_qb, 16)
     g.scalar.dma_start(T.bs[:], T.b[:]).then_inc(sem.ld_qb, 16)
 
@@ -52,18 +59,26 @@ def rank_program(g, core, T, topo):
     for j in partners:
         mask &= topo.mask(core, T.cores[j])
     eng = bin(mask).count("1")
-    own = T.kv[:, rank * W:(rank + 1) * W]
-    ids = []
-    for j in partners:
-        rid, pid = topo.addr(T.cores[j], core)
-        ids.append(DstId(rid=rid, pnc=pid))
-    g.wait_ge(sem.ld_kv, 32)
-    g.remote_dma_fused(
-        [RemoteDMATransfer(dst_ids=ids, dma_engine_mask=mask, remote_sem=sem["a%d" % rank],
-                           srcs=[own], dsts=[own for _ in partners])],
-        local_sem=sem.sent)
 
-    order = [rank] + partners
+    def send(ap, to, rsem, src=None):
+        ids = []
+        for j in to:
+            rid, pid = topo.addr(T.cores[j], core)
+            ids.append(DstId(rid=rid, pnc=pid))
+        g.remote_dma_fused(
+            [RemoteDMATransfer(dst_ids=ids, dma_engine_mask=mask, remote_sem=rsem, srcs=[ap if src is None else src],
+                               dsts=[ap for _ in to])],
+            local_sem=sem.sent)
+
+    g.wait_ge(sem.ld_kd, 16)
+    send(k_of(rank), [last], sem.ak, src=T.kd[:])
+    g.wait_ge(sem.ld_k, 16)
+    g.wait_ge(sem.ld_v, 16)
+    send(T.kv[:, rank * W:(rank + 1) * W], whole, sem["a%d" % rank])
+    send(v_of(rank), [last], sem.av)
+
+    order = [rank] + whole
+    M = len(order)
     banks = [T.p0, T.p1]
     acc = T.acc[:, 0:QP]
     ve.memset(T.zero[:], 0.0).then_inc(sem.vz, 1)
@@ -74,10 +89,16 @@ def rank_program(g, core, T, topo):
     for i, j in enumerate(order):
         ve.wait_ge(sem.pe1, i + 1)
         ve.tensor_tensor(cols(T.s, i), banks[i % 2][:, 0:QP], cols(T.nb, j), AluOpType.max).then_inc(sem.vmax, 1)
+        if i == 0:
+            ve.wait_ge(sem.peL, 1)
+            ve.tensor_tensor(T.tl[:], T.pl[:, 0:QP], cols(T.bs, last), AluOpType.add).then_inc(sem.vt, 1)
+            ve.wait_ge(sem.vt, 1)
+            ve.tensor_tensor(T.sl[:], T.tl[:], T.zero[:, 0:QP], AluOpType.max).then_inc(sem.vL, 1)
     ve.wait_ge(sem.pe2, 1)
     ve.tensor_copy(T.yo[:], acc).then_inc(sem.vy, 1)
 
-    pe.wait_ge(sem.ld_kv, 32)
+    pe.wait_ge(sem.ld_k, 16)
+    pe.wait_ge(sem.ld_v, 16)
     pe.wait_ge(sem.ld_qb, 32)
     for i, j in enumerate(order):
         if i > 0:
@@ -87,10 +108,16 @@ def rank_program(g, core, T, topo):
         if i > 0:
             pe.wait_ge(sem.vmax, i)
             pe.matmul(acc, v_of(order[i - 1]), cols(T.s, i - 1), start=False, stop=False)
-    pe.wait_ge(sem.vmax, N)
-    pe.matmul(acc, v_of(order[N - 1]), cols(T.s, N - 1), start=False, stop=True).then_inc(sem.pe2, 1)
+        if i == 0:
+            pe.wait_ge(sem.ak, eng)
+            pe.matmul(T.pl[:, 0:QP], k_of(last), T.qs[:], start=True, stop=True).then_inc(sem.peL, 1)
+    pe.wait_ge(sem.vmax, M)
+    pe.matmul(acc, v_of(order[M - 1]), cols(T.s, M - 1), start=False, stop=False)
+    pe.wait_ge(sem.vL, 1)
+    pe.wait_ge(sem.av, eng)
+    pe.matmul(acc, v_of(last), T.sl[:], start=False, stop=True).then_inc(sem.pe2, 1)
 
     g.sync.wait_ge(sem.vy, 1)
     g.sync.dma_start(T.y[:], T.yo[:]).then_inc(sem.st, 16)
     g.sync.wait_ge(sem.st, 16)
-    g.wait_ge(sem.sent, eng)
+    g.wait_ge(sem.sent, 3 * eng)

from concourse.bass import DstId, RemoteDMATransfer
from concourse.mybir import AluOpType

N = 8
QP = 32
KP = 128
W = 2 * KP

SCRATCH = {
    "kv": ("sbuf", [128, N * W], "bfloat16"),
    "kd": ("dram", [128, KP], "bfloat16"),
    "qs": ("sbuf", [128, QP], "bfloat16"),
    "bs": ("sbuf", [128, N * QP], "bfloat16"),
    "nb": ("sbuf", [128, N * QP], "bfloat16"),
    "zero": ("sbuf", [128, N * QP], "bfloat16"),
    "s": ("sbuf", [128, N * QP], "bfloat16"),
    "tl": ("sbuf", [128, QP], "float32"),
    "sl": ("sbuf", [128, QP], "bfloat16"),
    "yo": ("sbuf", [128, QP], "bfloat16"),
    "p0": ("psum", [128, 512], "float32"),
    "p1": ("psum", [128, 512], "float32"),
    "pl": ("psum", [128, 512], "float32"),
    "acc": ("psum", [128, 512], "float32"),
}
SEMAPHORES = ["ld_kd", "ld_k", "ld_v", "ld_qb", "sent", "vz", "vnb", "pe1", "vmax", "peL", "vt", "vL", "pe2", "vy", "st",
              "ak", "av"] + ["a%d" % j for j in range(N)]


def rank_program(g, core, T, topo):
    rank = T.rank_of(core)
    if rank is None:
        return
    sem = T.sem
    pe, ve = g.tensor, g.vector

    def k_of(j):
        return T.kv[:, j * W:j * W + KP]

    def v_of(j):
        return T.kv[:, j * W + KP:(j + 1) * W]

    def cols(t, j):
        return t[:, j * QP:(j + 1) * QP]

    def links(a, c):
        return 1 if (topo.mates(a, c) or topo.same_plane(a, c)) else 2

    steps = sorted(range(1, N), key=lambda t: (-links(core, T.cores[rank ^ t]), t))
    partners = [rank ^ t for t in steps]
    whole, last = partners[:-1], partners[-1]

    g.sync.dma_start(T.kd[:], T.k[:]).then_inc(sem.ld_kd, 16)
    g.scalar.dma_start(k_of(rank), T.k[:]).then_inc(sem.ld_k, 16)
    g.sync.dma_start(v_of(rank), T.v[:]).then_inc(sem.ld_v, 16)
    g.sync.dma_start(T.qs[:], T.q[:]).then_inc(sem.ld_qb, 16)
    g.scalar.dma_start(T.bs[:], T.b[:]).then_inc(sem.ld_qb, 16)

    mask = topo.mask(core, T.cores[partners[0]])
    for j in partners:
        mask &= topo.mask(core, T.cores[j])
    eng = bin(mask).count("1")

    def send(ap, to, rsem, src=None):
        ids = []
        for j in to:
            rid, pid = topo.addr(T.cores[j], core)
            ids.append(DstId(rid=rid, pnc=pid))
        g.remote_dma_fused(
            [RemoteDMATransfer(dst_ids=ids, dma_engine_mask=mask, remote_sem=rsem, srcs=[ap if src is None else src],
                               dsts=[ap for _ in to])],
            local_sem=sem.sent)

    g.wait_ge(sem.ld_kd, 16)
    send(k_of(rank), [last], sem.ak, src=T.kd[:])
    g.wait_ge(sem.ld_k, 16)
    g.wait_ge(sem.ld_v, 16)
    send(T.kv[:, rank * W:(rank + 1) * W], whole, sem["a%d" % rank])
    send(v_of(rank), [last], sem.av)

    order = [rank] + whole
    M = len(order)
    banks = [T.p0, T.p1]
    acc = T.acc[:, 0:QP]
    ve.memset(T.zero[:], 0.0).then_inc(sem.vz, 1)
    ve.wait_ge(sem.vz, 1)
    ve.wait_ge(sem.ld_qb, 32)
    ve.tensor_tensor(T.nb[:], T.zero[:], T.bs[:], AluOpType.subtract).then_inc(sem.vnb, 1)
    ve.wait_ge(sem.vnb, 1)
    for i, j in enumerate(order):
        ve.wait_ge(sem.pe1, i + 1)
        ve.tensor_tensor(cols(T.s, i), banks[i % 2][:, 0:QP], cols(T.nb, j), AluOpType.max).then_inc(sem.vmax, 1)
        if i == 0:
            ve.wait_ge(sem.peL, 1)
            ve.tensor_tensor(T.tl[:], T.pl[:, 0:QP], cols(T.bs, last), AluOpType.add).then_inc(sem.vt, 1)
            ve.wait_ge(sem.vt, 1)
            ve.tensor_tensor(T.sl[:], T.tl[:], T.zero[:, 0:QP], AluOpType.max).then_inc(sem.vL, 1)
    ve.wait_ge(sem.pe2, 1)
    ve.tensor_copy(T.yo[:], acc).then_inc(sem.vy, 1)

    pe.wait_ge(sem.ld_k, 16)
    pe.wait_ge(sem.ld_v, 16)
    pe.wait_ge(sem.ld_qb, 32)
    for i, j in enumerate(order):
        if i > 0:
            pe.wait_ge(sem["a%d" % j], eng)
        pe.matmul(banks[i % 2][:, 0:QP], k_of(j), T.qs[:], start=True, stop=True).then_inc(sem.pe1, 1)
        pe.matmul(acc, v_of(j), cols(T.bs, j), start=(i == 0), stop=False)
        if i > 0:
            pe.wait_ge(sem.vmax, i)
            pe.matmul(acc, v_of(order[i - 1]), cols(T.s, i - 1), start=False, stop=False)
        if i == 0:
            pe.wait_ge(sem.ak, eng)
            pe.matmul(T.pl[:, 0:QP], k_of(last), T.qs[:], start=True, stop=True).then_inc(sem.peL, 1)
    pe.wait_ge(sem.vmax, M)
    pe.matmul(acc, v_of(order[M - 1]), cols(T.s, M - 1), start=False, stop=False)
    pe.wait_ge(sem.vL, 1)
    pe.wait_ge(sem.av, eng)
    pe.matmul(acc, v_of(last), T.sl[:], start=False, stop=True).then_inc(sem.pe2, 1)

    g.sync.wait_ge(sem.vy, 1)
    g.sync.dma_start(T.y[:], T.yo[:]).then_inc(sem.st, 16)
    g.sync.wait_ge(sem.st, 16)
    g.wait_ge(sem.sent, 3 * eng)
